import numpy as np
import ml_dtypes


def mxq(x, axis, fmt="e4m3"):
    dtype, down = {"e4m3": (ml_dtypes.float8_e4m3fn, 7), "e5m2": (ml_dtypes.float8_e5m2, 14)}[fmt]
    v = np.moveaxis(np.asarray(x, np.float32).astype(ml_dtypes.bfloat16).astype(np.float64), axis, -1)
    blocks = v.reshape(v.shape[:-1] + (-1, 32))
    amax = np.abs(blocks).max(-1, keepdims=True)
    byte = np.maximum(np.where(amax > 0, np.frexp(amax)[1] - 1 + 127, 0) - down, 1)
    scale = np.exp2(byte - 127.0)
    codes = (blocks / scale).astype(np.float32).astype(dtype).astype(np.float64)
    return np.moveaxis((codes * scale).reshape(v.shape), -1, axis)


WIDE = False


def mx_kscale(k):
    if not WIDE:
        return np.ones(k)
    levels = np.array([30, -30])
    if k % 512:
        return np.exp2(np.random.permutation(np.resize(levels, k // 32))).repeat(32)
    a = np.empty((k // 512, 16))
    for p in range(k // 512):
        a[p, :8] = np.random.permutation(np.resize(levels, 8))
        for g in range(8):
            far = levels[np.abs(levels - a[p, g]) >= 10]
            a[p, g + 8] = far[np.random.randint(len(far))]
    return np.exp2(a.ravel()).repeat(32)


def f64(x):
    return np.asarray(x).astype(np.float64)


def striped(idx):
    return np.tile(np.asarray(idx).reshape(-1, 16).T, (8, 1)).astype(np.uint16)


def unstriped(offs):
    return offs[:16].T.reshape(-1).astype(np.int64)


E2M1 = np.array([0.0, 0.5, 1.0, 1.5, 2.0, 3.0, 4.0, 6.0, -0.0, -0.5, -1.0, -1.5, -2.0, -3.0, -4.0, -6.0])


def pack_weight(w, fmt):
    k, n = w.shape
    w = f64(np.asarray(w, np.float32).astype(ml_dtypes.bfloat16)).reshape(k // 32, 32, n)
    amax = np.abs(w).max(1)
    if fmt in ("e4m3", "e5m2"):
        byte = np.frexp(amax)[1] - 1 + 127 - (7 if fmt == "e4m3" else 14)
    else:
        mant, ex = np.frexp(amax / 6.0)
        byte = np.where(mant > 0.5, ex, ex - 1) + 127
    byte = np.clip(np.where(amax > 0, byte, 1), 1, 254)
    scaled = (w * np.exp2(127.0 - byte)[:, None, :]).reshape(k, n).astype(np.float32)
    by_word = np.ascontiguousarray(scaled.reshape(k // 512, 128, 4, n).transpose(0, 1, 3, 2))
    if fmt in ("e4m3", "e5m2"):
        words = by_word.astype(ml_dtypes.float8_e4m3fn if fmt == "e4m3" else ml_dtypes.float8_e5m2).view(np.uint8)
    else:
        c = by_word.astype(ml_dtypes.float4_e2m1fn).view(np.uint8) & 0xF
        words = (c[..., 0::2] | (c[..., 1::2] << 4)).reshape(k // 512, 128, 2 * n)
    return np.ascontiguousarray(words), np.ascontiguousarray(byte.astype(np.uint8).reshape(k // 512, 16, n))


def unpack_weight(words, scales, fmt):
    g, _, n = scales.shape
    words = np.ascontiguousarray(words).reshape(g, 128, n, -1)
    if fmt in ("e4m3", "e5m2"):
        vals = words.view(ml_dtypes.float8_e4m3fn if fmt == "e4m3" else ml_dtypes.float8_e5m2).astype(np.float64)
    else:
        nib = np.empty((g, 128, n, 4), np.uint8)
        nib[..., 0::2] = words & 0xF
        nib[..., 1::2] = words >> 4
        vals = E2M1[nib]
    vals = vals * np.repeat(np.exp2(scales.astype(np.float64) - 127.0), 8, axis=1)[..., None]
    return vals.transpose(0, 1, 3, 2).reshape(g * 512, n)


K, T, J, I, R, V = 512, 512, 256, 256, 512, 512


def setup_inputs():
    n = np.random.standard_normal
    idx = np.random.permutation(T)[:J]
    idx2 = np.random.permutation(V)[:J]
    idx3 = np.random.permutation(T)[:I]
    fk = mx_kscale(K)
    fr = mx_kscale(R)
    xtp = pack_weight(n((K, T)) / fk[:, None], "e5m2")
    wap = pack_weight(n((K, R)) * 0.5 / np.sqrt(K) * fk[:, None] * fr, "e2m1")
    wbp = pack_weight(n((K, R)) * 1 / np.sqrt(K) * fk[:, None] / fr, "e2m1")
    return {
        "xt_words": xtp[0],
        "xt_scales": xtp[1],
        "wa_words": wap[0],
        "wa_scales": wap[1],
        "tb": (n((R, V)) * 0.5 * fr[:, None]).astype(np.float32),
        "wb_words": wbp[0],
        "wb_scales": wbp[1],
        "offs": striped(idx),
        "offs2": striped(idx2),
        "offs3": striped(idx3),
    }


def reference(xt_words, xt_scales, wa_words, wa_scales, tb, wb_words, wb_scales, offs, offs2, offs3):
    idx = unstriped(offs)
    idx2 = unstriped(offs2)
    idx3 = unstriped(offs3)
    xtu = unpack_weight(xt_words, xt_scales, "e5m2")
    wau = unpack_weight(wa_words, wa_scales, "e2m1")
    wbu = unpack_weight(wb_words, wb_scales, "e2m1")
    xtidxg = xtu[:, idx]
    za = wau.T @ xtidxg
    ha = np.maximum(za - f64(tb)[:, idx2], 0.0)
    xtidx3g = xtu[:, idx3]
    zb = wbu.T @ xtidx3g
    kb1 = np.max(zb, axis=1, keepdims=True)
    hb = np.maximum(zb - 0.4 * kb1, 0.0)
    haq = mxq(ha, 0, "e5m2")
    hbq = mxq(hb, 0, "e5m2")
    a0 = haq.T @ hbq
    a1 = np.pad(a0, ((0, 0), (1, 0)))[:, :I]
    y = 0.04 * np.abs(a0 - a1)
    return y

@@ -1,0 +1,170 @@
+from contextlib import ExitStack
+
+import concourse.mybir as mybir
+
+K, T, J, I, R, V = 512, 512, 256, 256, 512, 512
+FLOPS = 2 * K * R * J + 2 * K * R * I + 2 * R * J * I
+
+F32 = mybir.dt.float32
+BF16 = mybir.dt.bfloat16
+I32 = mybir.dt.int32
+U32 = mybir.dt.uint32
+U16 = mybir.dt.uint16
+U8 = mybir.dt.uint8
+E5M2X4 = mybir.dt.float8_e5m2_x4
+E2M1X4 = mybir.dt.float4_e2m1fn_x4
+ALU = mybir.AluOpType
+ACT = mybir.ActivationFunctionType
+AX = mybir.AxisListType
+
+P = 128
+PACK = 4
+HALF = 128
+
+
+def tile_list_meet_overtable_peakgated_steps_kernel(
+    tc, xt_words, xt_scales, wa_words, wa_scales, tb, wb_words, wb_scales, offs, offs2, offs3, out
+):
+    nc = tc.nc
+    with ExitStack() as ctx:
+        sb = ctx.enter_context(tc.tile_pool(name="sb", bufs=1))
+        ps = ctx.enter_context(tc.psum_pool(name="ps", bufs=1))
+
+        def tile(shape, dtype, name):
+            return sb.tile(shape, dtype, name=name, align_bytes=64)
+
+        list_a = tile([P, J // 16], U16, "list_a")
+        list_t = tile([P, J // 16], U16, "list_t")
+        list_b = tile([P, I // 16], U16, "list_b")
+        x_words = tile([P, T], U32, "x_words")
+        x_scales = tile([P, T], U8, "x_scales")
+        raw_words = {n: tile([P, 2 * R], U8, "raw_words_" + n) for n in "ab"}
+        raw_scales = {n: tile([P, R], U8, "raw_scales_" + n) for n in "ab"}
+        w_words = {n: tile([P, 2 * R], U8, "w_words_" + n) for n in "ab"}
+        w_scales = {n: tile([P, R], U8, "w_scales_" + n) for n in "ab"}
+        table = [tile([P, V], F32, "table%d" % t) for t in range(PACK)]
+        shifted = [tile([P, I], F32, "shifted%d" % h) for h in range(2)]
+
+        nc.vector.memset(x_scales[:].bitcast(I32), 0)
+        nc.vector.memset(raw_scales["b"][:].bitcast(I32), 0)
+        nc.gpsimd.memset(raw_scales["a"][:].bitcast(I32), 0)
+        for h in range(2):
+            nc.gpsimd.memset(shifted[h][:, 0:1], 0.0)
+
+        def load_scales(queue, plane, src):
+            rows = src[0].bitcast(I32)
+            for q in range(4):
+                queue.dma_start(out=plane[32 * q : 32 * q + 4, :].bitcast(I32), in_=rows[4 * q : 4 * q + 4, :])
+
+        tb_rows = tb.rearrange("(g t q) v -> t g q v", t=PACK, q=8)
+
+        nc.sync.dma_start(list_b[:], offs3)
+        nc.sync.dma_start(out=x_words[:].bitcast(I32), in_=xt_words[0].rearrange("p n t -> p (n t)").bitcast(I32))
+        load_scales(nc.scalar, x_scales, xt_scales)
+        nc.sync.dma_start(list_a[:], offs)
+        nc.sync.dma_start(out=raw_words["b"][:].bitcast(I32), in_=wb_words[0].bitcast(I32))
+        load_scales(nc.sync, raw_scales["b"], wb_scales)
+        nc.sync.dma_start(out=table[0][:], in_=tb_rows[0])
+        nc.sync.dma_start(list_t[:], offs2)
+        nc.sync.dma_start(out=raw_words["a"][:].bitcast(I32), in_=wa_words[0].bitcast(I32))
+        load_scales(nc.sync, raw_scales["a"], wa_scales)
+        for t in range(1, PACK):
+            nc.sync.dma_start(out=table[t][:], in_=tb_rows[t])
+
+        def deal(n):
+            nc.scalar.copy(
+                out=w_words[n][:].bitcast(U32).rearrange("p (t g e) -> p t g e", t=PACK, e=4),
+                in_=raw_words[n][:].bitcast(U32).rearrange("p (g t e) -> p t g e", t=PACK, e=4),
+            )
+            nc.scalar.copy(
+                out=w_scales[n][:].bitcast(U32).rearrange("p (t g e) -> p t g e", t=PACK, e=2),
+                in_=raw_scales[n][:].bitcast(U32).rearrange("p (g t e) -> p t g e", t=PACK, e=2),
+            )
+
+        picked_words = {n: tile([P, J], U32, "picked_words_" + n) for n in "ab"}
+        picked_scales = {n: tile([P, J], U8, "picked_scales_" + n) for n in "ab"}
+        lists = {"a": list_a, "b": list_b}
+        z = {n: [ps.tile([P, PACK, HALF], F32, name="z%s%d" % (n, h)) for h in range(2)] for n in "ab"}
+
+        def first_stage(n):
+            nc.vector.tensor_copy(picked_words[n][:], x_words[:].indirect(lists[n][:]))
+            nc.vector.tensor_copy(picked_scales[n][:], x_scales[:].indirect(lists[n][:]))
+            deal(n)
+            for h in range(2):
+                cols = slice(h * HALF, (h + 1) * HALF)
+                for t in range(PACK):
+                    nc.tensor.matmul_mx(
+                        out=z[n][h][:, t, :],
+                        lhsT=w_words[n][:, 2 * P * t : 2 * P * (t + 1)].bitcast(E2M1X4),
+                        lhsT_scale=w_scales[n][:, P * t : P * (t + 1)],
+                        rhs=picked_words[n][:, cols].bitcast(E5M2X4),
+                        rhs_scale=picked_scales[n][:, cols],
+                        start=True,
+                        stop=True,
+                    )
+
+        first_stage("b")
+        first_stage("a")
+
+        picked_table = tile([P, PACK, J], F32, "picked_table")
+        for t in range(PACK):
+            nc.scalar.activation(picked_table[:, t, :], table[t][:].indirect(list_t[:]), ACT.Copy)
+
+        peaks = tile([P, 2, PACK], F32, "peaks")
+        peak = tile([P, PACK], F32, "peak")
+        for h in range(2):
+            nc.vector.tensor_reduce(out=peaks[:, h, :], in_=z["b"][h][:], axis=AX.X, op=ALU.max)
+        nc.vector.tensor_tensor(peak[:], peaks[:, 0, :], peaks[:, 1, :], ALU.max)
+
+        signed = {n: [tile([P, HALF, PACK], BF16, "signed_%s%d" % (n, h)) for h in range(2)] for n in "ab"}
+        hidden = {n: [tile([P, HALF * PACK], BF16, "hidden_%s%d" % (n, h)) for h in range(2)] for n in "ab"}
+        h_words = {n: tile([P, J], U32, "h_words_" + n) for n in "ab"}
+        h_scales = {n: tile([P, J], U8, "h_scales_" + n) for n in "ab"}
+
+        def quantise(n, h):
+            cols = slice(h * HALF, (h + 1) * HALF)
+            nc.vector.tensor_scalar_max(hidden[n][h][:], signed[n][h][:].rearrange("p c t -> p (c t)"), 0.0)
+            nc.vector.quantize_mx(
+                out=h_words[n][:, cols].bitcast(E5M2X4), scales=h_scales[n][:, cols], in_=hidden[n][h][:]
+            )
+
+        for h in range(2):
+            nc.vector.scalar_tensor_tensor(
+                out=signed["b"][h][:],
+                in0=peak[:].unsqueeze(1).to_broadcast([P, HALF, PACK]),
+                scalar=-0.4,
+                in1=z["b"][h][:].rearrange("p t c -> p c t"),
+                op0=ALU.mult,
+                op1=ALU.add,
+            )
+        for h in range(2):
+            quantise("b", h)
+        for h in range(2):
+            cols = slice(h * HALF, (h + 1) * HALF)
+            nc.vector.tensor_tensor(
+                signed["a"][h][:].rearrange("p (c i) t -> p c t i", i=4),
+                z["a"][h][:].rearrange("p t (c i) -> p c t i", i=4),
+                picked_table[:, :, cols].rearrange("p t (c i) -> p c t i", i=4),
+                ALU.subtract,
+            )
+        for h in range(2):
+            quantise("a", h)
+
+        for h in range(2):
+            cols = slice(h * HALF, (h + 1) * HALF)
+            scores = ps.tile([P, I], F32, name="scores%d" % h)
+            nc.tensor.matmul_mx(
+                out=scores[:],
+                lhsT=h_words["a"][:, cols].bitcast(E5M2X4),
+                lhsT_scale=h_scales["a"][:, cols],
+                rhs=h_words["b"][:].bitcast(E5M2X4),
+                rhs_scale=h_scales["b"][:],
+                start=True,
+                stop=True,
+            )
+            steps = tile([P, I], F32, "steps%d" % h)
+            result = tile([P, I], F32, "result%d" % h)
+            nc.scalar.copy(out=shifted[h][:, 1:I], in_=scores[:, 0 : I - 1])
+            nc.vector.tensor_tensor(steps[:], scores[:], shifted[h][:], ALU.subtract)
+            nc.scalar.activation(result[:], steps[:], ACT.Abs, scale=0.04)
+            nc.sync.dma_start(out=out[cols, :], in_=result[:])

@@ -45,16 +45,16 @@ def tile_list_meet_overtable_peakgated_steps_kernel(
         table = [tile([P, V], F32, "table%d" % t) for t in range(PACK)]
         shifted = [tile([P, I], F32, "shifted%d" % h) for h in range(2)]
 
-        nc.vector.memset(x_scales[:].bitcast(I32), 0)
-        nc.vector.memset(raw_scales["b"][:].bitcast(I32), 0)
-        nc.gpsimd.memset(raw_scales["a"][:].bitcast(I32), 0)
         for h in range(2):
             nc.gpsimd.memset(shifted[h][:, 0:1], 0.0)
 
         def load_scales(queue, plane, src):
-            rows = src[0].bitcast(I32)
+            rows = src.bitcast(I32)
             for q in range(4):
-                queue.dma_start(out=plane[32 * q : 32 * q + 4, :].bitcast(I32), in_=rows[4 * q : 4 * q + 4, :])
+                queue.dma_start(
+                    out=plane[32 * q : 32 * q + 32, :].bitcast(I32),
+                    in_=rows[:, 4 * q : 4 * q + 4, :].to_broadcast([8, 4, T // 4]),
+                )
 
         tb_rows = tb.rearrange("(g t q) v -> t g q v", t=PACK, q=8)
 
@@ -64,11 +64,12 @@ def tile_list_meet_overtable_peakgated_steps_kernel(
         nc.sync.dma_start(list_a[:], offs)
         nc.sync.dma_start(out=raw_words["b"][:].bitcast(I32), in_=wb_words[0].bitcast(I32))
         load_scales(nc.sync, raw_scales["b"], wb_scales)
-        nc.sync.dma_start(out=table[0][:], in_=tb_rows[0])
         nc.sync.dma_start(list_t[:], offs2)
         nc.sync.dma_start(out=raw_words["a"][:].bitcast(I32), in_=wa_words[0].bitcast(I32))
+        for t in range(2):
+            nc.sync.dma_start(out=table[t][:], in_=tb_rows[t])
         load_scales(nc.sync, raw_scales["a"], wa_scales)
-        for t in range(1, PACK):
+        for t in range(2, PACK):
             nc.sync.dma_start(out=table[t][:], in_=tb_rows[t])
 
         def deal(n):

@@ -30,8 +30,8 @@ def tile_list_meet_overtable_peakgated_steps_kernel(
         sb = ctx.enter_context(tc.tile_pool(name="sb", bufs=1))
         ps = ctx.enter_context(tc.psum_pool(name="ps", bufs=1))
 
-        def tile(shape, dtype, name):
-            return sb.tile(shape, dtype, name=name, align_bytes=64)
+        def tile(shape, dtype, name, tag=""):
+            return sb.tile(shape, dtype, name=name, tag=tag or name, align_bytes=64)
 
         list_a = tile([P, J // 16], U16, "list_a")
         list_t = tile([P, J // 16], U16, "list_t")
@@ -45,16 +45,16 @@ def tile_list_meet_overtable_peakgated_steps_kernel(
         table = [tile([P, V], F32, "table%d" % t) for t in range(PACK)]
         shifted = [tile([P, I], F32, "shifted%d" % h) for h in range(2)]
 
+        nc.gpsimd.memset(x_scales[:].bitcast(I32), 0)
+        for n in "ba":
+            nc.gpsimd.memset(raw_scales[n][:].bitcast(I32), 0)
         for h in range(2):
             nc.gpsimd.memset(shifted[h][:, 0:1], 0.0)
 
         def load_scales(queue, plane, src):
-            rows = src.bitcast(I32)
+            rows = src[0].bitcast(I32)
             for q in range(4):
-                queue.dma_start(
-                    out=plane[32 * q : 32 * q + 32, :].bitcast(I32),
-                    in_=rows[:, 4 * q : 4 * q + 4, :].to_broadcast([8, 4, T // 4]),
-                )
+                queue.dma_start(out=plane[32 * q : 32 * q + 4, :].bitcast(I32), in_=rows[4 * q : 4 * q + 4, :])
 
         tb_rows = tb.rearrange("(g t q) v -> t g q v", t=PACK, q=8)
 
@@ -64,12 +64,11 @@ def tile_list_meet_overtable_peakgated_steps_kernel(
         nc.sync.dma_start(list_a[:], offs)
         nc.sync.dma_start(out=raw_words["b"][:].bitcast(I32), in_=wb_words[0].bitcast(I32))
         load_scales(nc.sync, raw_scales["b"], wb_scales)
+        nc.sync.dma_start(out=table[0][:], in_=tb_rows[0])
         nc.sync.dma_start(list_t[:], offs2)
         nc.sync.dma_start(out=raw_words["a"][:].bitcast(I32), in_=wa_words[0].bitcast(I32))
-        for t in range(2):
-            nc.sync.dma_start(out=table[t][:], in_=tb_rows[t])
         load_scales(nc.sync, raw_scales["a"], wa_scales)
-        for t in range(2, PACK):
+        for t in range(1, PACK):
             nc.sync.dma_start(out=table[t][:], in_=tb_rows[t])
 
         def deal(n):
@@ -117,14 +116,20 @@ def tile_list_meet_overtable_peakgated_steps_kernel(
             nc.vector.tensor_reduce(out=peaks[:, h, :], in_=z["b"][h][:], axis=AX.X, op=ALU.max)
         nc.vector.tensor_tensor(peak[:], peaks[:, 0, :], peaks[:, 1, :], ALU.max)
 
-        signed = {n: [tile([P, HALF, PACK], BF16, "signed_%s%d" % (n, h)) for h in range(2)] for n in "ab"}
-        hidden = {n: [tile([P, HALF * PACK], BF16, "hidden_%s%d" % (n, h)) for h in range(2)] for n in "ab"}
+        signed = {n: [tile([P, HALF, PACK], F32 if n == "b" else BF16, "signed_%s%d" % (n, h)) for h in range(2)] for n in "ab"}
+        hidden = {n: [tile([P, HALF * PACK], BF16, "hidden_%s%d" % (n, h), "table3" if (n, h) == ("b", 0) else "") for h in range(2)] for n in "ab"}
         h_words = {n: tile([P, J], U32, "h_words_" + n) for n in "ab"}
         h_scales = {n: tile([P, J], U8, "h_scales_" + n) for n in "ab"}
 
+        def relu(n, h):
+            flat = signed[n][h][:].rearrange("p c t -> p (c t)")
+            if n == "b":
+                nc.scalar.activation(hidden[n][h][:], flat, ACT.Relu)
+            else:
+                nc.vector.tensor_scalar_max(hidden[n][h][:], flat, 0.0)
+
         def quantise(n, h):
             cols = slice(h * HALF, (h + 1) * HALF)
-            nc.vector.tensor_scalar_max(hidden[n][h][:], signed[n][h][:].rearrange("p c t -> p (c t)"), 0.0)
             nc.vector.quantize_mx(
                 out=h_words[n][:, cols].bitcast(E5M2X4), scales=h_scales[n][:, cols], in_=hidden[n][h][:]
             )
@@ -139,7 +144,7 @@ def tile_list_meet_overtable_peakgated_steps_kernel(
                 op1=ALU.add,
             )
         for h in range(2):
-            quantise("b", h)
+            relu("b", h)
         for h in range(2):
             cols = slice(h * HALF, (h + 1) * HALF)
             nc.vector.tensor_tensor(
@@ -149,7 +154,10 @@ def tile_list_meet_overtable_peakgated_steps_kernel(
                 ALU.subtract,
             )
         for h in range(2):
-            quantise("a", h)
+            relu("a", h)
+        for n in "ba":
+            for h in range(2):
+                quantise(n, h)
 
         for h in range(2):
             cols = slice(h * HALF, (h + 1) * HALF)

@@ -18,8 +18,15 @@ ACT = mybir.ActivationFunctionType
 AX = mybir.AxisListType
 
 P = 128
-PACK = 4
+PLANES = 4
+RUN = 8
+QUADRANTS = 4
+LIST_GROUP = 16
 HALF = 128
+HALVES = J // HALF
+LINE = 4
+GATE = 0.4
+OUT_SCALE = 0.04
 
 
 def tile_list_meet_overtable_peakgated_steps_kernel(
@@ -30,142 +37,125 @@ def tile_list_meet_overtable_peakgated_steps_kernel(
         sb = ctx.enter_context(tc.tile_pool(name="sb", bufs=1))
         ps = ctx.enter_context(tc.psum_pool(name="ps", bufs=1))
 
-        def tile(shape, dtype, name, tag=""):
-            return sb.tile(shape, dtype, name=name, tag=tag or name, align_bytes=64)
+        def tile(shape, dtype, name):
+            return sb.tile(shape, dtype, name=name, align_bytes=64)
 
-        list_a = tile([P, J // 16], U16, "list_a")
-        list_t = tile([P, J // 16], U16, "list_t")
-        list_b = tile([P, I // 16], U16, "list_b")
+        def half(h):
+            return slice(h * HALF, (h + 1) * HALF)
+
+        list_a = tile([P, J // LIST_GROUP], U16, "list_a")
+        list_t = tile([P, J // LIST_GROUP], U16, "list_t")
+        list_b = tile([P, I // LIST_GROUP], U16, "list_b")
         x_words = tile([P, T], U32, "x_words")
         x_scales = tile([P, T], U8, "x_scales")
         raw_words = {n: tile([P, 2 * R], U8, "raw_words_" + n) for n in "ab"}
         raw_scales = {n: tile([P, R], U8, "raw_scales_" + n) for n in "ab"}
         w_words = {n: tile([P, 2 * R], U8, "w_words_" + n) for n in "ab"}
         w_scales = {n: tile([P, R], U8, "w_scales_" + n) for n in "ab"}
-        table = [tile([P, V], F32, "table%d" % t) for t in range(PACK)]
-        shifted = [tile([P, I], F32, "shifted%d" % h) for h in range(2)]
+        table = [tile([P, V], F32, "table%d" % t) for t in range(PLANES)]
+        shifted = [tile([P, I], F32, "shifted%d" % h) for h in range(HALVES)]
 
         nc.gpsimd.memset(x_scales[:].bitcast(I32), 0)
         for n in "ba":
             nc.gpsimd.memset(raw_scales[n][:].bitcast(I32), 0)
-        for h in range(2):
+        for h in range(HALVES):
             nc.gpsimd.memset(shifted[h][:, 0:1], 0.0)
 
-        def load_scales(queue, plane, src):
+        def load_scales(queue, dst, src):
             rows = src[0].bitcast(I32)
-            for q in range(4):
-                queue.dma_start(out=plane[32 * q : 32 * q + 4, :].bitcast(I32), in_=rows[4 * q : 4 * q + 4, :])
+            for q in range(QUADRANTS):
+                queue.dma_start(out=dst[32 * q : 32 * q + 4, :].bitcast(I32), in_=rows[4 * q : 4 * q + 4, :])
 
-        tb_rows = tb.rearrange("(g t q) v -> t g q v", t=PACK, q=8)
-
+        tb_planes = tb.rearrange("(g t q) v -> t g q v", t=PLANES, q=RUN)
         nc.sync.dma_start(list_b[:], offs3)
         nc.sync.dma_start(out=x_words[:].bitcast(I32), in_=xt_words[0].rearrange("p n t -> p (n t)").bitcast(I32))
         load_scales(nc.scalar, x_scales, xt_scales)
         nc.sync.dma_start(list_a[:], offs)
         nc.sync.dma_start(out=raw_words["b"][:].bitcast(I32), in_=wb_words[0].bitcast(I32))
         load_scales(nc.sync, raw_scales["b"], wb_scales)
-        nc.sync.dma_start(out=table[0][:], in_=tb_rows[0])
+        nc.sync.dma_start(out=table[0][:], in_=tb_planes[0])
         nc.sync.dma_start(list_t[:], offs2)
         nc.sync.dma_start(out=raw_words["a"][:].bitcast(I32), in_=wa_words[0].bitcast(I32))
         load_scales(nc.sync, raw_scales["a"], wa_scales)
-        for t in range(1, PACK):
-            nc.sync.dma_start(out=table[t][:], in_=tb_rows[t])
+        for t in range(1, PLANES):
+            nc.sync.dma_start(out=table[t][:], in_=tb_planes[t])
 
-        def deal(n):
+        def sort_into_planes(dst, src):
             nc.scalar.copy(
-                out=w_words[n][:].bitcast(U32).rearrange("p (t g e) -> p t g e", t=PACK, e=4),
-                in_=raw_words[n][:].bitcast(U32).rearrange("p (g t e) -> p t g e", t=PACK, e=4),
-            )
-            nc.scalar.copy(
-                out=w_scales[n][:].bitcast(U32).rearrange("p (t g e) -> p t g e", t=PACK, e=2),
-                in_=raw_scales[n][:].bitcast(U32).rearrange("p (g t e) -> p t g e", t=PACK, e=2),
+                out=dst[:].bitcast(U32).rearrange("p (t g e) -> p t g e", t=PLANES, g=P // RUN),
+                in_=src[:].bitcast(U32).rearrange("p (g t e) -> p t g e", t=PLANES, g=P // RUN),
             )
 
         picked_words = {n: tile([P, J], U32, "picked_words_" + n) for n in "ab"}
         picked_scales = {n: tile([P, J], U8, "picked_scales_" + n) for n in "ab"}
         lists = {"a": list_a, "b": list_b}
-        z = {n: [ps.tile([P, PACK, HALF], F32, name="z%s%d" % (n, h)) for h in range(2)] for n in "ab"}
+        z = {n: [ps.tile([P, PLANES, HALF], F32, name="z%s%d" % (n, h)) for h in range(HALVES)] for n in "ab"}
 
-        def first_stage(n):
+        for n in "ba":
             nc.vector.tensor_copy(picked_words[n][:], x_words[:].indirect(lists[n][:]))
             nc.vector.tensor_copy(picked_scales[n][:], x_scales[:].indirect(lists[n][:]))
-            deal(n)
-            for h in range(2):
-                cols = slice(h * HALF, (h + 1) * HALF)
-                for t in range(PACK):
+            sort_into_planes(w_words[n], raw_words[n])
+            sort_into_planes(w_scales[n], raw_scales[n])
+            for h in range(HALVES):
+                for t in range(PLANES):
                     nc.tensor.matmul_mx(
                         out=z[n][h][:, t, :],
                         lhsT=w_words[n][:, 2 * P * t : 2 * P * (t + 1)].bitcast(E2M1X4),
                         lhsT_scale=w_scales[n][:, P * t : P * (t + 1)],
-                        rhs=picked_words[n][:, cols].bitcast(E5M2X4),
-                        rhs_scale=picked_scales[n][:, cols],
+                        rhs=picked_words[n][:, half(h)].bitcast(E5M2X4),
+                        rhs_scale=picked_scales[n][:, half(h)],
                         start=True,
                         stop=True,
                     )
 
-        first_stage("b")
-        first_stage("a")
-
-        picked_table = tile([P, PACK, J], F32, "picked_table")
-        for t in range(PACK):
+        picked_table = tile([P, PLANES, J], F32, "picked_table")
+        for t in range(PLANES):
             nc.scalar.activation(picked_table[:, t, :], table[t][:].indirect(list_t[:]), ACT.Copy)
 
-        peaks = tile([P, 2, PACK], F32, "peaks")
-        peak = tile([P, PACK], F32, "peak")
-        for h in range(2):
-            nc.vector.tensor_reduce(out=peaks[:, h, :], in_=z["b"][h][:], axis=AX.X, op=ALU.max)
-        nc.vector.tensor_tensor(peak[:], peaks[:, 0, :], peaks[:, 1, :], ALU.max)
+        half_peaks = tile([P, HALVES, PLANES], F32, "half_peaks")
+        peak = tile([P, PLANES], F32, "peak")
+        for h in range(HALVES):
+            nc.vector.tensor_reduce(out=half_peaks[:, h, :], in_=z["b"][h][:], axis=AX.X, op=ALU.max)
+        nc.vector.tensor_tensor(peak[:], half_peaks[:, 0, :], half_peaks[:, 1, :], ALU.max)
 
-        signed = {n: [tile([P, HALF, PACK], F32 if n == "b" else BF16, "signed_%s%d" % (n, h)) for h in range(2)] for n in "ab"}
-        hidden = {n: [tile([P, HALF * PACK], BF16, "hidden_%s%d" % (n, h), "table3" if (n, h) == ("b", 0) else "") for h in range(2)] for n in "ab"}
+        signed = {n: [tile([P, HALF, PLANES], BF16, "signed_%s%d" % (n, h)) for h in range(HALVES)] for n in "ab"}
+        hidden = {n: [tile([P, HALF * PLANES], BF16, "hidden_%s%d" % (n, h)) for h in range(HALVES)] for n in "ab"}
         h_words = {n: tile([P, J], U32, "h_words_" + n) for n in "ab"}
         h_scales = {n: tile([P, J], U8, "h_scales_" + n) for n in "ab"}
 
-        def relu(n, h):
-            flat = signed[n][h][:].rearrange("p c t -> p (c t)")
-            if n == "b":
-                nc.scalar.activation(hidden[n][h][:], flat, ACT.Relu)
-            else:
-                nc.vector.tensor_scalar_max(hidden[n][h][:], flat, 0.0)
-
-        def quantise(n, h):
-            cols = slice(h * HALF, (h + 1) * HALF)
+        def relu_and_quantise(n, h):
+            nc.vector.tensor_scalar_max(hidden[n][h][:], signed[n][h][:].rearrange("p c t -> p (c t)"), 0.0)
             nc.vector.quantize_mx(
-                out=h_words[n][:, cols].bitcast(E5M2X4), scales=h_scales[n][:, cols], in_=hidden[n][h][:]
+                out=h_words[n][:, half(h)].bitcast(E5M2X4), scales=h_scales[n][:, half(h)], in_=hidden[n][h][:]
             )
 
-        for h in range(2):
+        for h in range(HALVES):
             nc.vector.scalar_tensor_tensor(
                 out=signed["b"][h][:],
-                in0=peak[:].unsqueeze(1).to_broadcast([P, HALF, PACK]),
-                scalar=-0.4,
+                in0=peak[:].unsqueeze(1).to_broadcast([P, HALF, PLANES]),
+                scalar=-GATE,
                 in1=z["b"][h][:].rearrange("p t c -> p c t"),
                 op0=ALU.mult,
                 op1=ALU.add,
             )
-        for h in range(2):
-            relu("b", h)
-        for h in range(2):
-            cols = slice(h * HALF, (h + 1) * HALF)
+        for h in range(HALVES):
+            relu_and_quantise("b", h)
+        for h in range(HALVES):
             nc.vector.tensor_tensor(
-                signed["a"][h][:].rearrange("p (c i) t -> p c t i", i=4),
-                z["a"][h][:].rearrange("p t (c i) -> p c t i", i=4),
-                picked_table[:, :, cols].rearrange("p t (c i) -> p c t i", i=4),
+                signed["a"][h][:].rearrange("p (c i) t -> p c t i", i=LINE),
+                z["a"][h][:].rearrange("p t (c i) -> p c t i", i=LINE),
+                picked_table[:, :, half(h)].rearrange("p t (c i) -> p c t i", i=LINE),
                 ALU.subtract,
             )
-        for h in range(2):
-            relu("a", h)
-        for n in "ba":
-            for h in range(2):
-                quantise(n, h)
+        for h in range(HALVES):
+            relu_and_quantise("a", h)
 
-        for h in range(2):
-            cols = slice(h * HALF, (h + 1) * HALF)
+        for h in range(HALVES):
             scores = ps.tile([P, I], F32, name="scores%d" % h)
             nc.tensor.matmul_mx(
                 out=scores[:],
-                lhsT=h_words["a"][:, cols].bitcast(E5M2X4),
-                lhsT_scale=h_scales["a"][:, cols],
+                lhsT=h_words["a"][:, half(h)].bitcast(E5M2X4),
+                lhsT_scale=h_scales["a"][:, half(h)],
                 rhs=h_words["b"][:].bitcast(E5M2X4),
                 rhs_scale=h_scales["b"][:],
                 start=True,
@@ -175,5 +165,5 @@ def tile_list_meet_overtable_peakgated_steps_kernel(
             result = tile([P, I], F32, "result%d" % h)
             nc.scalar.copy(out=shifted[h][:, 1:I], in_=scores[:, 0 : I - 1])
             nc.vector.tensor_tensor(steps[:], scores[:], shifted[h][:], ALU.subtract)
-            nc.scalar.activation(result[:], steps[:], ACT.Abs, scale=0.04)
-            nc.sync.dma_start(out=out[cols, :], in_=result[:])
+            nc.scalar.activation(result[:], steps[:], ACT.Abs, scale=OUT_SCALE)
+            nc.sync.dma_start(out=out[half(h), :], in_=result[:])

from contextlib import ExitStack

import concourse.mybir as mybir

K, T, J, I, R, V = 512, 512, 256, 256, 512, 512
FLOPS = 2 * K * R * J + 2 * K * R * I + 2 * R * J * I

F32 = mybir.dt.float32
BF16 = mybir.dt.bfloat16
I32 = mybir.dt.int32
U32 = mybir.dt.uint32
U16 = mybir.dt.uint16
U8 = mybir.dt.uint8
E5M2X4 = mybir.dt.float8_e5m2_x4
E2M1X4 = mybir.dt.float4_e2m1fn_x4
ALU = mybir.AluOpType
ACT = mybir.ActivationFunctionType
AX = mybir.AxisListType

P = 128
PLANES = 4
RUN = 8
QUADRANTS = 4
LIST_GROUP = 16
HALF = 128
HALVES = J // HALF
LINE = 4
GATE = 0.4
OUT_SCALE = 0.04


def tile_list_meet_overtable_peakgated_steps_kernel(
    tc, xt_words, xt_scales, wa_words, wa_scales, tb, wb_words, wb_scales, offs, offs2, offs3, out
):
    nc = tc.nc
    with ExitStack() as ctx:
        sb = ctx.enter_context(tc.tile_pool(name="sb", bufs=1))
        ps = ctx.enter_context(tc.psum_pool(name="ps", bufs=1))

        def tile(shape, dtype, name):
            return sb.tile(shape, dtype, name=name, align_bytes=64)

        def half(h):
            return slice(h * HALF, (h + 1) * HALF)

        list_a = tile([P, J // LIST_GROUP], U16, "list_a")
        list_t = tile([P, J // LIST_GROUP], U16, "list_t")
        list_b = tile([P, I // LIST_GROUP], U16, "list_b")
        x_words = tile([P, T], U32, "x_words")
        x_scales = tile([P, T], U8, "x_scales")
        raw_words = {n: tile([P, 2 * R], U8, "raw_words_" + n) for n in "ab"}
        raw_scales = {n: tile([P, R], U8, "raw_scales_" + n) for n in "ab"}
        w_words = {n: tile([P, 2 * R], U8, "w_words_" + n) for n in "ab"}
        w_scales = {n: tile([P, R], U8, "w_scales_" + n) for n in "ab"}
        table = [tile([P, V], F32, "table%d" % t) for t in range(PLANES)]
        shifted = [tile([P, I], F32, "shifted%d" % h) for h in range(HALVES)]

        nc.gpsimd.memset(x_scales[:].bitcast(I32), 0)
        for n in "ba":
            nc.gpsimd.memset(raw_scales[n][:].bitcast(I32), 0)
        for h in range(HALVES):
            nc.gpsimd.memset(shifted[h][:, 0:1], 0.0)

        def load_scales(queue, dst, src):
            rows = src[0].bitcast(I32)
            for q in range(QUADRANTS):
                queue.dma_start(out=dst[32 * q : 32 * q + 4, :].bitcast(I32), in_=rows[4 * q : 4 * q + 4, :])

        tb_planes = tb.rearrange("(g t q) v -> t g q v", t=PLANES, q=RUN)
        nc.sync.dma_start(list_b[:], offs3)
        nc.sync.dma_start(out=x_words[:].bitcast(I32), in_=xt_words[0].rearrange("p n t -> p (n t)").bitcast(I32))
        load_scales(nc.scalar, x_scales, xt_scales)
        nc.sync.dma_start(list_a[:], offs)
        nc.sync.dma_start(out=raw_words["b"][:].bitcast(I32), in_=wb_words[0].bitcast(I32))
        load_scales(nc.sync, raw_scales["b"], wb_scales)
        nc.sync.dma_start(out=table[0][:], in_=tb_planes[0])
        nc.sync.dma_start(list_t[:], offs2)
        nc.sync.dma_start(out=raw_words["a"][:].bitcast(I32), in_=wa_words[0].bitcast(I32))
        load_scales(nc.sync, raw_scales["a"], wa_scales)
        for t in range(1, PLANES):
            nc.sync.dma_start(out=table[t][:], in_=tb_planes[t])

        def sort_into_planes(dst, src):
            nc.scalar.copy(
                out=dst[:].bitcast(U32).rearrange("p (t g e) -> p t g e", t=PLANES, g=P // RUN),
                in_=src[:].bitcast(U32).rearrange("p (g t e) -> p t g e", t=PLANES, g=P // RUN),
            )

        picked_words = {n: tile([P, J], U32, "picked_words_" + n) for n in "ab"}
        picked_scales = {n: tile([P, J], U8, "picked_scales_" + n) for n in "ab"}
        lists = {"a": list_a, "b": list_b}
        z = {n: [ps.tile([P, PLANES, HALF], F32, name="z%s%d" % (n, h)) for h in range(HALVES)] for n in "ab"}

        for n in "ba":
            nc.vector.tensor_copy(picked_words[n][:], x_words[:].indirect(lists[n][:]))
            nc.vector.tensor_copy(picked_scales[n][:], x_scales[:].indirect(lists[n][:]))
            sort_into_planes(w_words[n], raw_words[n])
            sort_into_planes(w_scales[n], raw_scales[n])
            for h in range(HALVES):
                for t in range(PLANES):
                    nc.tensor.matmul_mx(
                        out=z[n][h][:, t, :],
                        lhsT=w_words[n][:, 2 * P * t : 2 * P * (t + 1)].bitcast(E2M1X4),
                        lhsT_scale=w_scales[n][:, P * t : P * (t + 1)],
                        rhs=picked_words[n][:, half(h)].bitcast(E5M2X4),
                        rhs_scale=picked_scales[n][:, half(h)],
                        start=True,
                        stop=True,
                    )

        picked_table = tile([P, PLANES, J], F32, "picked_table")
        for t in range(PLANES):
            nc.scalar.activation(picked_table[:, t, :], table[t][:].indirect(list_t[:]), ACT.Copy)

        half_peaks = tile([P, HALVES, PLANES], F32, "half_peaks")
        peak = tile([P, PLANES], F32, "peak")
        for h in range(HALVES):
            nc.vector.tensor_reduce(out=half_peaks[:, h, :], in_=z["b"][h][:], axis=AX.X, op=ALU.max)
        nc.vector.tensor_tensor(peak[:], half_peaks[:, 0, :], half_peaks[:, 1, :], ALU.max)

        signed = {n: [tile([P, HALF, PLANES], BF16, "signed_%s%d" % (n, h)) for h in range(HALVES)] for n in "ab"}
        hidden = {n: [tile([P, HALF * PLANES], BF16, "hidden_%s%d" % (n, h)) for h in range(HALVES)] for n in "ab"}
        h_words = {n: tile([P, J], U32, "h_words_" + n) for n in "ab"}
        h_scales = {n: tile([P, J], U8, "h_scales_" + n) for n in "ab"}

        def relu_and_quantise(n, h):
            nc.vector.tensor_scalar_max(hidden[n][h][:], signed[n][h][:].rearrange("p c t -> p (c t)"), 0.0)
            nc.vector.quantize_mx(
                out=h_words[n][:, half(h)].bitcast(E5M2X4), scales=h_scales[n][:, half(h)], in_=hidden[n][h][:]
            )

        for h in range(HALVES):
            nc.vector.scalar_tensor_tensor(
                out=signed["b"][h][:],
                in0=peak[:].unsqueeze(1).to_broadcast([P, HALF, PLANES]),
                scalar=-GATE,
                in1=z["b"][h][:].rearrange("p t c -> p c t"),
                op0=ALU.mult,
                op1=ALU.add,
            )
        for h in range(HALVES):
            relu_and_quantise("b", h)
        for h in range(HALVES):
            nc.vector.tensor_tensor(
                signed["a"][h][:].rearrange("p (c i) t -> p c t i", i=LINE),
                z["a"][h][:].rearrange("p t (c i) -> p c t i", i=LINE),
                picked_table[:, :, half(h)].rearrange("p t (c i) -> p c t i", i=LINE),
                ALU.subtract,
            )
        for h in range(HALVES):
            relu_and_quantise("a", h)

        for h in range(HALVES):
            scores = ps.tile([P, I], F32, name="scores%d" % h)
            nc.tensor.matmul_mx(
                out=scores[:],
                lhsT=h_words["a"][:, half(h)].bitcast(E5M2X4),
                lhsT_scale=h_scales["a"][:, half(h)],
                rhs=h_words["b"][:].bitcast(E5M2X4),
                rhs_scale=h_scales["b"][:],
                start=True,
                stop=True,
            )
            steps = tile([P, I], F32, "steps%d" % h)
            result = tile([P, I], F32, "result%d" % h)
            nc.scalar.copy(out=shifted[h][:, 1:I], in_=scores[:, 0 : I - 1])
            nc.vector.tensor_tensor(steps[:], scores[:], shifted[h][:], ALU.subtract)
            nc.scalar.activation(result[:], steps[:], ACT.Abs, scale=OUT_SCALE)
            nc.sync.dma_start(out=out[half(h), :], in_=result[:])
